import numpy as np
import ml_dtypes


def mxq(x, axis, fmt="e4m3"):
    dtype, down = {"e4m3": (ml_dtypes.float8_e4m3fn, 7), "e5m2": (ml_dtypes.float8_e5m2, 14)}[fmt]
    v = np.moveaxis(np.asarray(x, np.float32).astype(ml_dtypes.bfloat16).astype(np.float64), axis, -1)
    blocks = v.reshape(v.shape[:-1] + (-1, 32))
    amax = np.abs(blocks).max(-1, keepdims=True)
    byte = np.maximum(np.where(amax > 0, np.frexp(amax)[1] - 1 + 127, 0) - down, 1)
    scale = np.exp2(byte - 127.0)
    codes = (blocks / scale).astype(np.float32).astype(dtype).astype(np.float64)
    return np.moveaxis((codes * scale).reshape(v.shape), -1, axis)


WIDE = False


def mx_kscale(k):
    if not WIDE:
        return np.ones(k)
    levels = np.array([10, -10, 5, -5, 0])
    if k % 512:
        return np.exp2(np.random.permutation(np.resize(levels, k // 32))).repeat(32)
    a = np.empty((k // 512, 16))
    for p in range(k // 512):
        a[p, :8] = np.random.permutation(np.resize(levels, 8))
        for g in range(8):
            far = levels[np.abs(levels - a[p, g]) >= 10]
            a[p, g + 8] = far[np.random.randint(len(far))]
    return np.exp2(a.ravel()).repeat(32)


def f64(x):
    return np.asarray(x).astype(np.float64)


def striped(idx):
    return np.tile(idx.reshape(-1, 16).T, (8, 1)).astype(np.uint16)


def unstriped(offs):
    return offs[:16].T.reshape(-1).astype(np.int64)


def striped8(idx):
    return np.concatenate([x.reshape(-1, 16).T for x in idx]).astype(np.uint16)


def runs(offs, k):
    lists = np.stack([offs[16 * r : 16 * r + 16].T.reshape(-1) for r in range(8)]).astype(np.int64)
    return lists[np.arange(k) % 512 // 64]


def pack_weight(w):
    k, n = w.shape
    w = f64(np.asarray(w, np.float32).astype(ml_dtypes.bfloat16)).reshape(k // 32, 32, n)
    amax = np.abs(w).max(1)
    byte = np.clip(np.where(amax > 0, np.frexp(amax)[1] - 1 + 127 - 7, 1), 1, 254)
    scaled = (w * np.exp2(127.0 - byte)[:, None, :]).reshape(k, n).astype(np.float32)
    words = np.ascontiguousarray(scaled.reshape(k // 512, 128, 4, n).transpose(0, 1, 3, 2)).astype(ml_dtypes.float8_e4m3fn).view(np.uint8)
    return words, np.ascontiguousarray(byte.astype(np.uint8).reshape(k // 512, 16, n))


def unpack_weight(words, scales):
    g, p, n, _ = words.shape
    vals = np.ascontiguousarray(words).view(ml_dtypes.float8_e4m3fn).astype(np.float64) * np.repeat(np.exp2(scales.astype(np.float64) - 127.0), 8, axis=1)[..., None]
    return vals.transpose(0, 1, 3, 2).reshape(g * 512, n)


E2M1 = np.array([0.0, 0.5, 1.0, 1.5, 2.0, 3.0, 4.0, 6.0, -0.0, -0.5, -1.0, -1.5, -2.0, -3.0, -4.0, -6.0])


def pack_fp4(w):
    k, n = w.shape
    w = f64(np.asarray(w, np.float32).astype(ml_dtypes.bfloat16)).reshape(k // 32, 32, n)
    amax = np.abs(w).max(1)
    mant, ex = np.frexp(amax / 6.0)
    byte = np.clip(np.where(amax > 0, np.where(mant > 0.5, ex, ex - 1) + 127, 1), 1, 254)
    scaled = (w * np.exp2(127.0 - byte)[:, None, :]).reshape(k, n).astype(np.float32)
    c = np.ascontiguousarray(scaled.reshape(k // 512, 128, 4, n).transpose(0, 1, 3, 2)).astype(ml_dtypes.float4_e2m1fn).view(np.uint8) & 0xF
    words = (c[..., 0::2] | (c[..., 1::2] << 4)).reshape(k // 512, 128, 2 * n)
    return np.ascontiguousarray(words), np.ascontiguousarray(byte.astype(np.uint8).reshape(k // 512, 16, n))


def unpack_fp4(words, scales):
    g, _, n = scales.shape
    words = np.ascontiguousarray(words).reshape(g, 128, n, 2)
    nib = np.empty((g, 128, n, 4), np.uint8)
    nib[..., 0::2] = words & 0xF
    nib[..., 1::2] = words >> 4
    vals = E2M1[nib] * np.repeat(np.exp2(scales.astype(np.float64) - 127.0), 8, axis=1)[..., None]
    return vals.transpose(0, 1, 3, 2).reshape(g * 512, n)


def sigmoid(v):
    return 1.0 / (1.0 + np.exp(-np.maximum(v, -700.0)))

def planes(y):
    n, m = y.shape
    v = y.astype(np.float32).astype(ml_dtypes.bfloat16).astype(np.float64).reshape(n // 32, 32, m)
    top = np.abs(v).max(1)
    byte = np.clip(np.where(top > 0, np.frexp(top)[1] - 1 + 127 - 7, 1), 1, 254)
    codes = (v * np.exp2(127.0 - byte)[:, None, :]).reshape(n, m).astype(np.float32).astype(ml_dtypes.float8_e4m3fn).view(np.uint8)
    words = codes.reshape(n // 512, 128, 4, m).transpose(0, 1, 3, 2)
    return np.ascontiguousarray(words), np.ascontiguousarray(byte.astype(np.uint8).reshape(n // 512, 16, m))


K, T, S, N, H = 512, 2048, 512, 512, 512


def setup_inputs():
    n = np.random.standard_normal
    s = mx_kscale(K)[:, None]
    u = mx_kscale(H)
    packed_xT = pack_weight(n((K, T)) * s)
    packed_w1 = pack_fp4(n((K, H)) / np.sqrt(K) / s)
    packed_w2 = pack_fp4(n((H, N)) / np.sqrt(H) / u[:, None])
    return {
        "x_words": packed_xT[0],
        "x_scales": packed_xT[1],
        "w1_words": packed_w1[0],
        "w1_scales": packed_w1[1],
        "gn": (np.random.uniform(0.5, 1.5, (H, 1)) * u[:, None]).astype(np.float32),
        "w2_words": packed_w2[0],
        "w2_scales": packed_w2[1],
        "offs": striped(np.random.permutation(T)[:S]),
        "n1": striped8(np.stack([np.random.permutation(S) for _ in range(8)])),
        "n2": striped8(np.stack([np.random.permutation(S) for _ in range(8)])),
        "n3": striped8(np.stack([np.random.permutation(S) for _ in range(8)])),
        "n4": striped8(np.stack([np.random.permutation(S) for _ in range(8)])),
    }


def reference(x_words, x_scales, w1_words, w1_scales, gn, w2_words, w2_scales, offs, n1, n2, n3, n4):
    xq = unpack_weight(x_words, x_scales)[:, unstriped(offs)]
    y = unpack_fp4(w1_words, w1_scales).T @ xq
    z = f64(gn) * (y[np.arange(H)[:, None], runs(n1, H)] - (y[np.arange(H)[:, None], runs(n2, H)]))
    h = unpack_fp4(w2_words, w2_scales).T @ mxq(z, 0, "e4m3")
    out_0 = (h + h[np.arange(N)[:, None], runs(n3, N)]) * (sigmoid(y + y[np.arange(H)[:, None], runs(n4, H)]))
    return (out_0,) + planes(out_0)

@@ -1,0 +1,264 @@
+from contextlib import ExitStack
+
+import concourse.mybir as mybir
+from concourse.masks import make_identity
+
+K, T, S, N, H = 512, 2048, 512, 512, 512
+FLOPS = 2 * K * H * S + 2 * H * N * S
+
+F32 = mybir.dt.float32
+BF16 = mybir.dt.bfloat16
+I32 = mybir.dt.int32
+U32 = mybir.dt.uint32
+U16 = mybir.dt.uint16
+U8 = mybir.dt.uint8
+FP8X4 = mybir.dt.float8_e4m3fn_x4
+FP4X4 = mybir.dt.float4_e2m1fn_x4
+ALU = mybir.AluOpType
+ACT = mybir.ActivationFunctionType
+
+P = 128
+PACK = 4
+HALF = S // 2
+OUT_CHUNKS = ((0, 256), (256, 128), (384, 128))
+
+
+def picked(window, offsets, start, width):
+    return window[:].indirect(offsets[:, start // 16 : (start + width) // 16])
+
+
+def load_scale_rows(queue, plane, rows):
+    for q in range(4):
+        queue.dma_start(out=plane[32 * q : 32 * q + 4, :].bitcast(I32), in_=rows[4 * q : 4 * q + 4, :].bitcast(I32))
+
+
+def tile_picked_skiptriebgap_none_po_kernel(
+    tc, x_words, x_scales, w1_words, w1_scales, gn, w2_words, w2_scales, offs, n1, n2, n3, n4, out_0, out_1, out_2
+):
+    nc = tc.nc
+    with ExitStack() as ctx:
+        lists = ctx.enter_context(tc.tile_pool(name="lists", bufs=1))
+        sb = ctx.enter_context(tc.tile_pool(name="sb", bufs=1))
+        ps = ctx.enter_context(tc.psum_pool(name="ps", bufs=1))
+
+        def new(shape, dtype, name, tag=None):
+            return sb.tile(shape, dtype, name=name, tag=tag or name, align_bytes=64)
+
+        offs_sb = lists.tile([P, S // 16], U16, name="offs_sb")
+        n1_sb = lists.tile([P, S // 16], U16, name="n1_sb")
+        n2_sb = lists.tile([P, S // 16], U16, name="n2_sb")
+        n3_sb = lists.tile([P, S // 16], U16, name="n3_sb")
+        n4_sb = lists.tile([P, S // 16], U16, name="n4_sb")
+
+        xw_all = new([P, T], U32, "xw_all")
+        xs_all = new([P, T], U8, "xs_all")
+        w1w_raw = new([P, 2 * H], U8, "w1w_raw")
+        w2w_raw = new([P, 2 * N], U8, "w2w_raw")
+        w1s_raw = new([P, H], U8, "w1s_raw")
+        w2s_raw = new([P, N], U8, "w2s_raw")
+        gain = new([P, PACK], F32, "gain")
+        ident = new([P, P], F32, "ident")
+
+        nc.vector.memset(xs_all[:].bitcast(I32), 0)
+        nc.gpsimd.memset(w1s_raw[:].bitcast(I32), 0)
+        nc.gpsimd.memset(w2s_raw[:].bitcast(I32), 0)
+
+        nc.sync.dma_start(offs_sb[:], offs)
+        nc.sync.dma_start(out=w1w_raw[:].bitcast(I32), in_=w1_words[0].bitcast(I32))
+        load_scale_rows(nc.sync, xs_all, x_scales[0])
+        nc.sync.dma_start(out=xw_all[:].bitcast(I32), in_=x_words[0].rearrange("p c r -> p (c r)").bitcast(I32))
+        load_scale_rows(nc.sync, w1s_raw, w1_scales[0])
+        nc.sync.dma_start(n2_sb[:], n2)
+        nc.sync.dma_start(n1_sb[:], n1)
+        nc.sync.dma_start(out=gain[:], in_=gn.rearrange("(p t) o -> p (t o)", t=PACK))
+        nc.sync.dma_start(n4_sb[:], n4)
+        nc.sync.dma_start(n3_sb[:], n3)
+        nc.gpsimd.dma_start(out=w2w_raw[:].bitcast(I32), in_=w2_words[0].bitcast(I32))
+        load_scale_rows(nc.gpsimd, w2s_raw, w2_scales[0])
+        make_identity(nc, ident[:])
+
+        xs = new([P, S], U8, "xs")
+        nc.vector.tensor_copy(out=xs[:], in_=picked(xs_all, offs_sb, 0, S))
+
+        w1w = new([P, 2 * H], U8, "w1w")
+        w1s = new([P, H], U8, "w1s")
+        w2w = new([P, 2 * N], U8, "w2w")
+
+        def deal_words(dst, src):
+            nc.scalar.copy(
+                out=dst[:].bitcast(U16).rearrange("p (t m) -> p t m", t=PACK),
+                in_=src[:].bitcast(U16).rearrange("p (m t) -> p t m", t=PACK),
+            )
+
+        def deal_scales(engine, dst, src):
+            engine.tensor_copy(
+                out=dst[:].rearrange("p (t m) -> p t m", t=PACK),
+                in_=src[:].rearrange("p (m t) -> p t m", t=PACK),
+            )
+
+        deal_words(w1w, w1w_raw)
+        xw = [new([P, HALF], U32, f"xw{a}") for a in range(2)]
+        for a in range(2):
+            nc.vector.tensor_copy(out=xw[a][:], in_=picked(xw_all, offs_sb, a * HALF, HALF))
+            if a == 0:
+                deal_scales(nc.vector, w1s, w1s_raw)
+        deal_words(w2w, w2w_raw)
+
+        def product(out, words, scales, t, rhs_words, rhs_scales):
+            nc.tensor.matmul_mx(
+                out=out,
+                lhsT=words[:, 2 * P * t : 2 * P * (t + 1)].bitcast(FP4X4),
+                lhsT_scale=scales[:, P * t : P * (t + 1)],
+                rhs=rhs_words.bitcast(FP8X4),
+                rhs_scale=rhs_scales,
+                start=True,
+                stop=True,
+            )
+
+        def half_banks(name, a):
+            banks = [ps.tile([P, 2, HALF], F32, name=f"{name}{a}{e}", tag=f"bank{2 * a + e}") for e in range(2)]
+            return banks
+
+        y = [new([P, S], F32, f"y{t}") for t in range(PACK)]
+
+        def y_product(out, t, a):
+            product(out, w1w, w1s, t, xw[a][:], xs[:, a * HALF : (a + 1) * HALF])
+
+        for a in range(2):
+            cols = slice(a * HALF, (a + 1) * HALF)
+            banks = [ps.tile([P, HALF], F32, name=f"y_ps{t}{a}", tag=f"bank{4 * (1 - a) + t}") for t in range(2)]
+            for t in range(2):
+                y_product(banks[t][:], t, a)
+            nc.scalar.activation(out=y[0][:, cols], in_=banks[0][:], func=ACT.Copy)
+            nc.vector.tensor_copy(out=y[1][:, cols], in_=banks[1][:])
+        for t in range(2, PACK):
+            bank = ps.tile([P, S], F32, name=f"y_ps{t}", tag=f"bank{t}")
+            for a in range(2):
+                y_product(bank[:, a * HALF : (a + 1) * HALF], t, a)
+            nc.vector.tensor_copy(out=y[t][:], in_=bank[:])
+
+        w2s = new([P, N], U8, "w2s", "w1s")
+        h = [new([P, S], F32, f"h{t}") for t in range(PACK)]
+        gain_b = gain[:].unsqueeze(1).unsqueeze(3).broadcast_to([P, HALF // 4, PACK, 4])
+        h_ps = []
+        for a in range(2):
+            y_n2 = new([P, PACK, HALF], F32, f"y_n2_{a}")
+            diff = new([P, PACK, HALF], F32, f"diff{a}")
+            for t in range(PACK):
+                nc.scalar.activation(out=y_n2[:, t, :], in_=picked(y[t], n2_sb, a * HALF, HALF), func=ACT.Copy)
+                nc.vector.tensor_tensor(
+                    out=diff[:, t, :], in0=picked(y[t], n1_sb, a * HALF, HALF), in1=y_n2[:, t, :], op=ALU.subtract
+                )
+            if a == 0:
+                deal_scales(nc.vector, w2s, w2s_raw)
+            z_bf = new([P, HALF * PACK], BF16, f"z_bf{a}")
+            nc.vector.tensor_tensor(
+                out=z_bf[:].rearrange("p (c i t) -> p c t i", i=4, t=PACK),
+                in0=diff[:].rearrange("p t (c i) -> p c t i", i=4),
+                in1=gain_b,
+                op=ALU.mult,
+            )
+            zw = new([P, HALF], U32, f"zw{a}")
+            zs = new([P, HALF], U8, f"zs{a}")
+            nc.vector.quantize_mx(out=zw[:].bitcast(FP8X4), scales=zs[:], in_=z_bf[:])
+            h_ps.append(half_banks("h_ps", a))
+            for t in range(PACK):
+                product(h_ps[a][t % 2][:, t // 2, :], w2w, w2s, t, zw[:], zs[:])
+
+        for a in range(2):
+            for t in range(PACK):
+                dst, src = h[t][:, a * HALF : (a + 1) * HALF], h_ps[a][t % 2][:, t // 2, :]
+                if a == 1 and t % 2 == 0:
+                    nc.scalar.activation(out=dst, in_=src, func=ACT.Copy, scale=0.5)
+                else:
+                    nc.vector.tensor_scalar(out=dst, in0=src, scalar1=0.5, scalar2=None, op0=ALU.mult)
+
+        y_n4 = {}
+
+        def gather_n4(a, planes, tag):
+            tile = new([P, len(planes), HALF], F32, f"y_n4_{a}{planes[0]}", tag)
+            for i, t in enumerate(planes):
+                y_n4[t, a] = tile[:, i, :]
+                nc.scalar.activation(out=y_n4[t, a], in_=picked(y[t], n4_sb, a * HALF, HALF), func=ACT.Copy)
+
+        gate_ps = {}
+
+        def gate(c, gate_tag):
+            a, b = divmod(c, 2)
+            sum_ps = ps.tile([P, PACK, P], F32, name=f"sum_ps{c}", tag=f"bank{4 + c}")
+            for t in range(PACK):
+                nc.tensor.matmul(
+                    sum_ps[:, t, :], lhsT=y[t][:, c * P : (c + 1) * P], rhs=ident[:],
+                    is_transpose=True, start=(t == 0), stop=False,
+                )
+            for t in (range(PACK) if a == 0 else reversed(range(PACK))):
+                nc.tensor.matmul(
+                    sum_ps[:, t, :], lhsT=y_n4[t, a][:, b * P : (b + 1) * P], rhs=ident[:],
+                    is_transpose=True, start=False, stop=(t == (PACK - 1 if a == 0 else 0)),
+                )
+            gate_t = new([P, PACK, P], F32, f"gate_t{c}", gate_tag)
+            nc.scalar.activation(out=gate_t[:], in_=sum_ps[:], func=ACT.Tanh, scale=0.5)
+            gate_ps[c] = ps.tile([P, PACK, P], F32, name=f"gate_ps{c}", tag=f"bank{4 + c}")
+            for t in range(PACK):
+                nc.tensor.transpose(gate_ps[c][:, t, :], gate_t[:, t, :], ident[:])
+
+        out_rows = out_0.rearrange("(p t) c -> p t c", t=PACK)
+        out_words = out_1[0].rearrange("p c r -> p (c r)").bitcast(I32)
+        o_scales = new([P, S], U8, "o_scales")
+        h_n3 = {}
+
+        def gather_n3(start, width, planes, on_vector, tag=None):
+            if start not in h_n3:
+                h_n3[start] = new([P, PACK, width], F32, f"h_n3_{start}", tag)
+            for t in planes:
+                if on_vector:
+                    nc.vector.tensor_copy(out=h_n3[start][:, t, :], in_=picked(h[t], n3_sb, start, width))
+                else:
+                    nc.scalar.activation(out=h_n3[start][:, t, :], in_=picked(h[t], n3_sb, start, width), func=ACT.Copy)
+
+        def finish(start, width, parities):
+            a, off = divmod(start, HALF)
+            h_sum = new([P, PACK, width], F32, f"h_sum{start}")
+            for e in parities:
+                nc.vector.scalar_tensor_tensor(
+                    out=h_sum[:, e::2, :], in0=h_ps[a][e][:, :, off : off + width], scalar=0.5,
+                    in1=h_n3[start][:, e::2, :], op0=ALU.mult, op1=ALU.add,
+                )
+            o32 = new([P, PACK, width], F32, f"o32_{start}")
+            for b in range(width // P):
+                nc.vector.scalar_tensor_tensor(
+                    out=o32[:, :, b * P : (b + 1) * P], in0=gate_ps[start // P + b][:], scalar=1.0,
+                    in1=h_sum[:, :, b * P : (b + 1) * P], op0=ALU.add, op1=ALU.mult,
+                )
+            nc.sync.dma_start(out=out_rows[:, :, start : start + width], in_=o32[:])
+            o_bf = new([P, width * PACK], BF16, f"o_bf{start}")
+            nc.vector.tensor_copy(
+                out=o_bf[:].rearrange("p (c i t) -> p c t i", i=4, t=PACK),
+                in_=o32[:].rearrange("p t (c i) -> p c t i", i=4),
+            )
+            o_words = new([P, width], U32, f"o_words{start}")
+            nc.vector.quantize_mx(
+                out=o_words[:].bitcast(FP8X4), scales=o_scales[:, start : start + width], in_=o_bf[:]
+            )
+            nc.sync.dma_start(out=out_words[:, start : start + width], in_=o_words[:].bitcast(I32))
+
+        gather_n4(0, (0, 1, 2, 3), None)
+        gate(0, None)
+        gather_n4(1, (0, 1), None)
+        gather_n3(0, HALF, (1, 3), True)
+        gather_n3(0, HALF, (0, 2), False)
+        gate(1, "zs1")
+        finish(0, HALF, (1, 0))
+        gather_n4(1, (2, 3), "zw1")
+        gather_n3(HALF, P, (0, 2), False)
+        gate(2, None)
+        gather_n3(HALF, P, (1, 3), False)
+        gate(3, None)
+        finish(HALF, P, (0, 1))
+        gather_n3(HALF + P, P, (0, 2, 1, 3), False, "zw1")
+        finish(HALF + P, P, (0, 1))
+        for q in range(4):
+            queue = nc.sync if q % 2 == 0 else nc.scalar
+            queue.dma_start(
+                out=out_2[0][4 * q : 4 * q + 4, :].bitcast(I32), in_=o_scales[32 * q : 32 * q + 4, :].bitcast(I32)
+            )

@@ -20,7 +20,6 @@ ACT = mybir.ActivationFunctionType
 P = 128
 PACK = 4
 HALF = S // 2
-OUT_CHUNKS = ((0, 256), (256, 128), (384, 128))
 
 
 def picked(window, offsets, start, width):
@@ -68,12 +67,12 @@ def tile_picked_skiptriebgap_none_po_kernel(
         load_scale_rows(nc.sync, xs_all, x_scales[0])
         nc.sync.dma_start(out=xw_all[:].bitcast(I32), in_=x_words[0].rearrange("p c r -> p (c r)").bitcast(I32))
         load_scale_rows(nc.sync, w1s_raw, w1_scales[0])
+        nc.sync.dma_start(out=w2w_raw[:].bitcast(I32), in_=w2_words[0].bitcast(I32))
         nc.sync.dma_start(n2_sb[:], n2)
         nc.sync.dma_start(n1_sb[:], n1)
         nc.sync.dma_start(out=gain[:], in_=gn.rearrange("(p t) o -> p (t o)", t=PACK))
         nc.sync.dma_start(n4_sb[:], n4)
         nc.sync.dma_start(n3_sb[:], n3)
-        nc.gpsimd.dma_start(out=w2w_raw[:].bitcast(I32), in_=w2_words[0].bitcast(I32))
         load_scale_rows(nc.gpsimd, w2s_raw, w2_scales[0])
         make_identity(nc, ident[:])
 
@@ -97,8 +96,9 @@ def tile_picked_skiptriebgap_none_po_kernel(
             )
 
         deal_words(w1w, w1w_raw)
-        xw = [new([P, HALF], U32, f"xw{a}") for a in range(2)]
+        xw = []
         for a in range(2):
+            xw.append(new([P, HALF], U32, f"xw{a}", "w1s_raw" if a == 1 else None))
             nc.vector.tensor_copy(out=xw[a][:], in_=picked(xw_all, offs_sb, a * HALF, HALF))
             if a == 0:
                 deal_scales(nc.vector, w1s, w1s_raw)
@@ -137,20 +137,19 @@ def tile_picked_skiptriebgap_none_po_kernel(
                 y_product(bank[:, a * HALF : (a + 1) * HALF], t, a)
             nc.vector.tensor_copy(out=y[t][:], in_=bank[:])
 
-        w2s = new([P, N], U8, "w2s", "w1s")
+        w2s = new([P, N], U8, "w2s", "xw_all")
+        deal_scales(nc.gpsimd, w2s, w2s_raw)
         h = [new([P, S], F32, f"h{t}") for t in range(PACK)]
         gain_b = gain[:].unsqueeze(1).unsqueeze(3).broadcast_to([P, HALF // 4, PACK, 4])
         h_ps = []
         for a in range(2):
-            y_n2 = new([P, PACK, HALF], F32, f"y_n2_{a}")
             diff = new([P, PACK, HALF], F32, f"diff{a}")
             for t in range(PACK):
-                nc.scalar.activation(out=y_n2[:, t, :], in_=picked(y[t], n2_sb, a * HALF, HALF), func=ACT.Copy)
+                y_n2 = new([P, HALF], F32, f"y_n2_{t}{a}", f"y_n2_{t}")
+                nc.scalar.activation(out=y_n2[:], in_=picked(y[t], n2_sb, a * HALF, HALF), func=ACT.Copy)
                 nc.vector.tensor_tensor(
-                    out=diff[:, t, :], in0=picked(y[t], n1_sb, a * HALF, HALF), in1=y_n2[:, t, :], op=ALU.subtract
+                    out=diff[:, t, :], in0=picked(y[t], n1_sb, a * HALF, HALF), in1=y_n2[:], op=ALU.subtract
                 )
-            if a == 0:
-                deal_scales(nc.vector, w2s, w2s_raw)
             z_bf = new([P, HALF * PACK], BF16, f"z_bf{a}")
             nc.vector.tensor_tensor(
                 out=z_bf[:].rearrange("p (c i t) -> p c t i", i=4, t=PACK),
@@ -162,28 +161,31 @@ def tile_picked_skiptriebgap_none_po_kernel(
             zs = new([P, HALF], U8, f"zs{a}")
             nc.vector.quantize_mx(out=zw[:].bitcast(FP8X4), scales=zs[:], in_=z_bf[:])
             h_ps.append(half_banks("h_ps", a))
-            for t in range(PACK):
+            for t in (0, 2, 1, 3):
                 product(h_ps[a][t % 2][:, t // 2, :], w2w, w2s, t, zw[:], zs[:])
 
-        for a in range(2):
-            for t in range(PACK):
-                dst, src = h[t][:, a * HALF : (a + 1) * HALF], h_ps[a][t % 2][:, t // 2, :]
-                if a == 1 and t % 2 == 0:
-                    nc.scalar.activation(out=dst, in_=src, func=ACT.Copy, scale=0.5)
-                else:
-                    nc.vector.tensor_scalar(out=dst, in0=src, scalar1=0.5, scalar2=None, op0=ALU.mult)
+        h_first = new([P, PACK, HALF], F32, "h_first")
+        for e in range(2):
+            nc.scalar.activation(out=h_first[:, e::2, :], in_=h_ps[0][e][:], func=ACT.Copy, scale=0.5)
+            for t in (e, e + 2):
+                nc.sync.dma_start(out=h[t][:, :HALF], in_=h_first[:, t, :])
+        for t in (0, 2, 1, 3):
+            nc.scalar.activation(out=h[t][:, HALF:], in_=h_ps[1][t % 2][:, t // 2, :], func=ACT.Copy, scale=0.5)
 
         y_n4 = {}
 
-        def gather_n4(a, planes, tag):
-            tile = new([P, len(planes), HALF], F32, f"y_n4_{a}{planes[0]}", tag)
-            for i, t in enumerate(planes):
+        def gather_n4(pieces, tag, on_vector):
+            tile = new([P, len(pieces), HALF], F32, f"y_n4_{pieces[0][0]}{pieces[0][1]}", tag)
+            for i, (t, a) in enumerate(pieces):
                 y_n4[t, a] = tile[:, i, :]
-                nc.scalar.activation(out=y_n4[t, a], in_=picked(y[t], n4_sb, a * HALF, HALF), func=ACT.Copy)
+                if on_vector:
+                    nc.vector.tensor_copy(out=y_n4[t, a], in_=picked(y[t], n4_sb, a * HALF, HALF))
+                else:
+                    nc.scalar.activation(out=y_n4[t, a], in_=picked(y[t], n4_sb, a * HALF, HALF), func=ACT.Copy)
 
         gate_ps = {}
 
-        def gate(c, gate_tag):
+        def gate(c):
             a, b = divmod(c, 2)
             sum_ps = ps.tile([P, PACK, P], F32, name=f"sum_ps{c}", tag=f"bank{4 + c}")
             for t in range(PACK):
@@ -191,72 +193,82 @@ def tile_picked_skiptriebgap_none_po_kernel(
                     sum_ps[:, t, :], lhsT=y[t][:, c * P : (c + 1) * P], rhs=ident[:],
                     is_transpose=True, start=(t == 0), stop=False,
                 )
-            for t in (range(PACK) if a == 0 else reversed(range(PACK))):
+            order = list(reversed(range(PACK)))
+            for t in order:
                 nc.tensor.matmul(
                     sum_ps[:, t, :], lhsT=y_n4[t, a][:, b * P : (b + 1) * P], rhs=ident[:],
-                    is_transpose=True, start=False, stop=(t == (PACK - 1 if a == 0 else 0)),
+                    is_transpose=True, start=False, stop=(t == order[-1]),
                 )
-            gate_t = new([P, PACK, P], F32, f"gate_t{c}", gate_tag)
+            gate_t = new([P, PACK, P], F32, f"gate_t{c}")
             nc.scalar.activation(out=gate_t[:], in_=sum_ps[:], func=ACT.Tanh, scale=0.5)
             gate_ps[c] = ps.tile([P, PACK, P], F32, name=f"gate_ps{c}", tag=f"bank{4 + c}")
             for t in range(PACK):
                 nc.tensor.transpose(gate_ps[c][:, t, :], gate_t[:, t, :], ident[:])
 
+        gather_n4([(0, 0), (1, 0), (2, 0)], "y_n2_0", False)
+        gather_n4([(3, 0)], "z_bf0", False)
+        gather_n4([(3, 1), (2, 1), (1, 1)], "z_bf1", True)
+        gate(0)
+        gate(1)
+        gather_n4([(0, 1)], "zw0", False)
+
         out_rows = out_0.rearrange("(p t) c -> p t c", t=PACK)
         out_words = out_1[0].rearrange("p c r -> p (c r)").bitcast(I32)
         o_scales = new([P, S], U8, "o_scales")
-        h_n3 = {}
+        h_sum = [new([P, PACK, HALF], F32, f"h_sum{a}") for a in range(2)]
+        o32 = [new([P, PACK, HALF], F32, f"o32_{a}") for a in range(2)]
+        o_bf = [new([P, HALF * PACK], BF16, f"o_bf{a}") for a in range(2)]
 
-        def gather_n3(start, width, planes, on_vector, tag=None):
-            if start not in h_n3:
-                h_n3[start] = new([P, PACK, width], F32, f"h_n3_{start}", tag)
-            for t in planes:
-                if on_vector:
-                    nc.vector.tensor_copy(out=h_n3[start][:, t, :], in_=picked(h[t], n3_sb, start, width))
-                else:
-                    nc.scalar.activation(out=h_n3[start][:, t, :], in_=picked(h[t], n3_sb, start, width), func=ACT.Copy)
-
-        def finish(start, width, parities):
-            a, off = divmod(start, HALF)
-            h_sum = new([P, PACK, width], F32, f"h_sum{start}")
-            for e in parities:
-                nc.vector.scalar_tensor_tensor(
-                    out=h_sum[:, e::2, :], in0=h_ps[a][e][:, :, off : off + width], scalar=0.5,
-                    in1=h_n3[start][:, e::2, :], op0=ALU.mult, op1=ALU.add,
-                )
-            o32 = new([P, PACK, width], F32, f"o32_{start}")
-            for b in range(width // P):
-                nc.vector.scalar_tensor_tensor(
-                    out=o32[:, :, b * P : (b + 1) * P], in0=gate_ps[start // P + b][:], scalar=1.0,
-                    in1=h_sum[:, :, b * P : (b + 1) * P], op0=ALU.add, op1=ALU.mult,
-                )
-            nc.sync.dma_start(out=out_rows[:, :, start : start + width], in_=o32[:])
-            o_bf = new([P, width * PACK], BF16, f"o_bf{start}")
-            nc.vector.tensor_copy(
-                out=o_bf[:].rearrange("p (c i t) -> p c t i", i=4, t=PACK),
-                in_=o32[:].rearrange("p t (c i) -> p c t i", i=4),
+        def gated(c):
+            a, b = divmod(c, 2)
+            cols = slice(b * P, (b + 1) * P)
+            nc.vector.scalar_tensor_tensor(
+                out=o32[a][:, :, cols], in0=gate_ps[c][:], scalar=1.0, in1=h_sum[a][:, :, cols],
+                op0=ALU.add, op1=ALU.mult,
             )
-            o_words = new([P, width], U32, f"o_words{start}")
-            nc.vector.quantize_mx(
-                out=o_words[:].bitcast(FP8X4), scales=o_scales[:, start : start + width], in_=o_bf[:]
-            )
-            nc.sync.dma_start(out=out_words[:, start : start + width], in_=o_words[:].bitcast(I32))
 
-        gather_n4(0, (0, 1, 2, 3), None)
-        gate(0, None)
-        gather_n4(1, (0, 1), None)
-        gather_n3(0, HALF, (1, 3), True)
-        gather_n3(0, HALF, (0, 2), False)
-        gate(1, "zs1")
-        finish(0, HALF, (1, 0))
-        gather_n4(1, (2, 3), "zw1")
-        gather_n3(HALF, P, (0, 2), False)
-        gate(2, None)
-        gather_n3(HALF, P, (1, 3), False)
-        gate(3, None)
-        finish(HALF, P, (0, 1))
-        gather_n3(HALF + P, P, (0, 2, 1, 3), False, "zw1")
-        finish(HALF + P, P, (0, 1))
+        def rounded(a, start, width, on_vector):
+            dst = o_bf[a][:, PACK * start : PACK * (start + width)].rearrange("p (c i t) -> p c t i", i=4, t=PACK)
+            src = o32[a][:, :, start : start + width].rearrange("p t (c i) -> p c t i", i=4)
+            if on_vector:
+                nc.vector.tensor_copy(out=dst, in_=src)
+            else:
+                nc.scalar.copy(out=dst, in_=src)
+
+        def planes(a):
+            cols = slice(a * HALF, (a + 1) * HALF)
+            o_words = new([P, HALF], U32, f"o_words{a}")
+            nc.vector.quantize_mx(out=o_words[:].bitcast(FP8X4), scales=o_scales[:, cols], in_=o_bf[a][:])
+            nc.sync.dma_start(out=out_words[:, cols], in_=o_words[:].bitcast(I32))
+
+        for t in (0, 2, 1, 3):
+            nc.vector.tensor_tensor(
+                out=h_sum[0][:, t, :], in0=picked(h[t], n3_sb, 0, HALF), in1=h_first[:, t, :], op=ALU.add
+            )
+        gated(0)
+        gated(1)
+        nc.sync.dma_start(out=out_rows[:, :, :HALF], in_=o32[0][:])
+
+        h_n3 = new([P, PACK, HALF], F32, "h_n3")
+        for t in (0, 2, 1, 3):
+            nc.scalar.activation(out=h_n3[:, t, :], in_=picked(h[t], n3_sb, HALF, HALF), func=ACT.Copy)
+        gate(2)
+        gate(3)
+        for e in range(2):
+            nc.vector.scalar_tensor_tensor(
+                out=h_sum[1][:, e::2, :], in0=h_ps[1][e][:], scalar=0.5, in1=h_n3[:, e::2, :],
+                op0=ALU.mult, op1=ALU.add,
+            )
+        rounded(0, 0, HALF, False)
+        for b in range(2):
+            gated(2 + b)
+            nc.sync.dma_start(
+                out=out_rows[:, :, HALF + b * P : HALF + (b + 1) * P], in_=o32[1][:, :, b * P : (b + 1) * P]
+            )
+        rounded(1, 0, P, False)
+        planes(0)
+        rounded(1, P, P, True)
+        planes(1)
         for q in range(4):
             queue = nc.sync if q % 2 == 0 else nc.scalar
             queue.dma_start(

@@ -254,11 +254,12 @@ def tile_picked_skiptriebgap_none_po_kernel(
             nc.scalar.activation(out=h_n3[:, t, :], in_=picked(h[t], n3_sb, HALF, HALF), func=ACT.Copy)
         gate(2)
         gate(3)
-        for e in range(2):
-            nc.vector.scalar_tensor_tensor(
-                out=h_sum[1][:, e::2, :], in0=h_ps[1][e][:], scalar=0.5, in1=h_n3[:, e::2, :],
-                op0=ALU.mult, op1=ALU.add,
-            )
+        nc.vector.scalar_tensor_tensor(
+            out=h_sum[1][:, 0::2, :], in0=h_ps[1][0][:], scalar=0.5, in1=h_n3[:, 0::2, :],
+            op0=ALU.mult, op1=ALU.add,
+        )
+        for t in (1, 3):
+            nc.gpsimd.tensor_tensor(out=h_sum[1][:, t, :], in0=h_n3[:, t, :], in1=h[t][:, HALF:], op=ALU.add)
         rounded(0, 0, HALF, False)
         for b in range(2):
             gated(2 + b)

from contextlib import ExitStack

import concourse.mybir as mybir
from concourse.masks import make_identity

K, T, S, N, H = 512, 2048, 512, 512, 512
FLOPS = 2 * K * H * S + 2 * H * N * S

F32 = mybir.dt.float32
BF16 = mybir.dt.bfloat16
I32 = mybir.dt.int32
U32 = mybir.dt.uint32
U16 = mybir.dt.uint16
U8 = mybir.dt.uint8
FP8X4 = mybir.dt.float8_e4m3fn_x4
FP4X4 = mybir.dt.float4_e2m1fn_x4
ALU = mybir.AluOpType
ACT = mybir.ActivationFunctionType

P = 128
PACK = 4
HALF = S // 2


def picked(window, offsets, start, width):
    return window[:].indirect(offsets[:, start // 16 : (start + width) // 16])


def load_scale_rows(queue, plane, rows):
    for q in range(4):
        queue.dma_start(out=plane[32 * q : 32 * q + 4, :].bitcast(I32), in_=rows[4 * q : 4 * q + 4, :].bitcast(I32))


def tile_picked_skiptriebgap_none_po_kernel(
    tc, x_words, x_scales, w1_words, w1_scales, gn, w2_words, w2_scales, offs, n1, n2, n3, n4, out_0, out_1, out_2
):
    nc = tc.nc
    with ExitStack() as ctx:
        lists = ctx.enter_context(tc.tile_pool(name="lists", bufs=1))
        sb = ctx.enter_context(tc.tile_pool(name="sb", bufs=1))
        ps = ctx.enter_context(tc.psum_pool(name="ps", bufs=1))

        def new(shape, dtype, name, tag=None):
            return sb.tile(shape, dtype, name=name, tag=tag or name, align_bytes=64)

        offs_sb = lists.tile([P, S // 16], U16, name="offs_sb")
        n1_sb = lists.tile([P, S // 16], U16, name="n1_sb")
        n2_sb = lists.tile([P, S // 16], U16, name="n2_sb")
        n3_sb = lists.tile([P, S // 16], U16, name="n3_sb")
        n4_sb = lists.tile([P, S // 16], U16, name="n4_sb")

        xw_all = new([P, T], U32, "xw_all")
        xs_all = new([P, T], U8, "xs_all")
        w1w_raw = new([P, 2 * H], U8, "w1w_raw")
        w2w_raw = new([P, 2 * N], U8, "w2w_raw")
        w1s_raw = new([P, H], U8, "w1s_raw")
        w2s_raw = new([P, N], U8, "w2s_raw")
        gain = new([P, PACK], F32, "gain")
        ident = new([P, P], F32, "ident")

        nc.vector.memset(xs_all[:].bitcast(I32), 0)
        nc.gpsimd.memset(w1s_raw[:].bitcast(I32), 0)
        nc.gpsimd.memset(w2s_raw[:].bitcast(I32), 0)

        nc.sync.dma_start(offs_sb[:], offs)
        nc.sync.dma_start(out=w1w_raw[:].bitcast(I32), in_=w1_words[0].bitcast(I32))
        load_scale_rows(nc.sync, xs_all, x_scales[0])
        nc.sync.dma_start(out=xw_all[:].bitcast(I32), in_=x_words[0].rearrange("p c r -> p (c r)").bitcast(I32))
        load_scale_rows(nc.sync, w1s_raw, w1_scales[0])
        nc.sync.dma_start(out=w2w_raw[:].bitcast(I32), in_=w2_words[0].bitcast(I32))
        nc.sync.dma_start(n2_sb[:], n2)
        nc.sync.dma_start(n1_sb[:], n1)
        nc.sync.dma_start(out=gain[:], in_=gn.rearrange("(p t) o -> p (t o)", t=PACK))
        nc.sync.dma_start(n4_sb[:], n4)
        nc.sync.dma_start(n3_sb[:], n3)
        load_scale_rows(nc.gpsimd, w2s_raw, w2_scales[0])
        make_identity(nc, ident[:])

        xs = new([P, S], U8, "xs")
        nc.vector.tensor_copy(out=xs[:], in_=picked(xs_all, offs_sb, 0, S))

        w1w = new([P, 2 * H], U8, "w1w")
        w1s = new([P, H], U8, "w1s")
        w2w = new([P, 2 * N], U8, "w2w")

        def deal_words(dst, src):
            nc.scalar.copy(
                out=dst[:].bitcast(U16).rearrange("p (t m) -> p t m", t=PACK),
                in_=src[:].bitcast(U16).rearrange("p (m t) -> p t m", t=PACK),
            )

        def deal_scales(engine, dst, src):
            engine.tensor_copy(
                out=dst[:].rearrange("p (t m) -> p t m", t=PACK),
                in_=src[:].rearrange("p (m t) -> p t m", t=PACK),
            )

        deal_words(w1w, w1w_raw)
        xw = []
        for a in range(2):
            xw.append(new([P, HALF], U32, f"xw{a}", "w1s_raw" if a == 1 else None))
            nc.vector.tensor_copy(out=xw[a][:], in_=picked(xw_all, offs_sb, a * HALF, HALF))
            if a == 0:
                deal_scales(nc.vector, w1s, w1s_raw)
        deal_words(w2w, w2w_raw)

        def product(out, words, scales, t, rhs_words, rhs_scales):
            nc.tensor.matmul_mx(
                out=out,
                lhsT=words[:, 2 * P * t : 2 * P * (t + 1)].bitcast(FP4X4),
                lhsT_scale=scales[:, P * t : P * (t + 1)],
                rhs=rhs_words.bitcast(FP8X4),
                rhs_scale=rhs_scales,
                start=True,
                stop=True,
            )

        def half_banks(name, a):
            banks = [ps.tile([P, 2, HALF], F32, name=f"{name}{a}{e}", tag=f"bank{2 * a + e}") for e in range(2)]
            return banks

        y = [new([P, S], F32, f"y{t}") for t in range(PACK)]

        def y_product(out, t, a):
            product(out, w1w, w1s, t, xw[a][:], xs[:, a * HALF : (a + 1) * HALF])

        for a in range(2):
            cols = slice(a * HALF, (a + 1) * HALF)
            banks = [ps.tile([P, HALF], F32, name=f"y_ps{t}{a}", tag=f"bank{4 * (1 - a) + t}") for t in range(2)]
            for t in range(2):
                y_product(banks[t][:], t, a)
            nc.scalar.activation(out=y[0][:, cols], in_=banks[0][:], func=ACT.Copy)
            nc.vector.tensor_copy(out=y[1][:, cols], in_=banks[1][:])
        for t in range(2, PACK):
            bank = ps.tile([P, S], F32, name=f"y_ps{t}", tag=f"bank{t}")
            for a in range(2):
                y_product(bank[:, a * HALF : (a + 1) * HALF], t, a)
            nc.vector.tensor_copy(out=y[t][:], in_=bank[:])

        w2s = new([P, N], U8, "w2s", "xw_all")
        deal_scales(nc.gpsimd, w2s, w2s_raw)
        h = [new([P, S], F32, f"h{t}") for t in range(PACK)]
        gain_b = gain[:].unsqueeze(1).unsqueeze(3).broadcast_to([P, HALF // 4, PACK, 4])
        h_ps = []
        for a in range(2):
            diff = new([P, PACK, HALF], F32, f"diff{a}")
            for t in range(PACK):
                y_n2 = new([P, HALF], F32, f"y_n2_{t}{a}", f"y_n2_{t}")
                nc.scalar.activation(out=y_n2[:], in_=picked(y[t], n2_sb, a * HALF, HALF), func=ACT.Copy)
                nc.vector.tensor_tensor(
                    out=diff[:, t, :], in0=picked(y[t], n1_sb, a * HALF, HALF), in1=y_n2[:], op=ALU.subtract
                )
            z_bf = new([P, HALF * PACK], BF16, f"z_bf{a}")
            nc.vector.tensor_tensor(
                out=z_bf[:].rearrange("p (c i t) -> p c t i", i=4, t=PACK),
                in0=diff[:].rearrange("p t (c i) -> p c t i", i=4),
                in1=gain_b,
                op=ALU.mult,
            )
            zw = new([P, HALF], U32, f"zw{a}")
            zs = new([P, HALF], U8, f"zs{a}")
            nc.vector.quantize_mx(out=zw[:].bitcast(FP8X4), scales=zs[:], in_=z_bf[:])
            h_ps.append(half_banks("h_ps", a))
            for t in (0, 2, 1, 3):
                product(h_ps[a][t % 2][:, t // 2, :], w2w, w2s, t, zw[:], zs[:])

        h_first = new([P, PACK, HALF], F32, "h_first")
        for e in range(2):
            nc.scalar.activation(out=h_first[:, e::2, :], in_=h_ps[0][e][:], func=ACT.Copy, scale=0.5)
            for t in (e, e + 2):
                nc.sync.dma_start(out=h[t][:, :HALF], in_=h_first[:, t, :])
        for t in (0, 2, 1, 3):
            nc.scalar.activation(out=h[t][:, HALF:], in_=h_ps[1][t % 2][:, t // 2, :], func=ACT.Copy, scale=0.5)

        y_n4 = {}

        def gather_n4(pieces, tag, on_vector):
            tile = new([P, len(pieces), HALF], F32, f"y_n4_{pieces[0][0]}{pieces[0][1]}", tag)
            for i, (t, a) in enumerate(pieces):
                y_n4[t, a] = tile[:, i, :]
                if on_vector:
                    nc.vector.tensor_copy(out=y_n4[t, a], in_=picked(y[t], n4_sb, a * HALF, HALF))
                else:
                    nc.scalar.activation(out=y_n4[t, a], in_=picked(y[t], n4_sb, a * HALF, HALF), func=ACT.Copy)

        gate_ps = {}

        def gate(c):
            a, b = divmod(c, 2)
            sum_ps = ps.tile([P, PACK, P], F32, name=f"sum_ps{c}", tag=f"bank{4 + c}")
            for t in range(PACK):
                nc.tensor.matmul(
                    sum_ps[:, t, :], lhsT=y[t][:, c * P : (c + 1) * P], rhs=ident[:],
                    is_transpose=True, start=(t == 0), stop=False,
                )
            order = list(reversed(range(PACK)))
            for t in order:
                nc.tensor.matmul(
                    sum_ps[:, t, :], lhsT=y_n4[t, a][:, b * P : (b + 1) * P], rhs=ident[:],
                    is_transpose=True, start=False, stop=(t == order[-1]),
                )
            gate_t = new([P, PACK, P], F32, f"gate_t{c}")
            nc.scalar.activation(out=gate_t[:], in_=sum_ps[:], func=ACT.Tanh, scale=0.5)
            gate_ps[c] = ps.tile([P, PACK, P], F32, name=f"gate_ps{c}", tag=f"bank{4 + c}")
            for t in range(PACK):
                nc.tensor.transpose(gate_ps[c][:, t, :], gate_t[:, t, :], ident[:])

        gather_n4([(0, 0), (1, 0), (2, 0)], "y_n2_0", False)
        gather_n4([(3, 0)], "z_bf0", False)
        gather_n4([(3, 1), (2, 1), (1, 1)], "z_bf1", True)
        gate(0)
        gate(1)
        gather_n4([(0, 1)], "zw0", False)

        out_rows = out_0.rearrange("(p t) c -> p t c", t=PACK)
        out_words = out_1[0].rearrange("p c r -> p (c r)").bitcast(I32)
        o_scales = new([P, S], U8, "o_scales")
        h_sum = [new([P, PACK, HALF], F32, f"h_sum{a}") for a in range(2)]
        o32 = [new([P, PACK, HALF], F32, f"o32_{a}") for a in range(2)]
        o_bf = [new([P, HALF * PACK], BF16, f"o_bf{a}") for a in range(2)]

        def gated(c):
            a, b = divmod(c, 2)
            cols = slice(b * P, (b + 1) * P)
            nc.vector.scalar_tensor_tensor(
                out=o32[a][:, :, cols], in0=gate_ps[c][:], scalar=1.0, in1=h_sum[a][:, :, cols],
                op0=ALU.add, op1=ALU.mult,
            )

        def rounded(a, start, width, on_vector):
            dst = o_bf[a][:, PACK * start : PACK * (start + width)].rearrange("p (c i t) -> p c t i", i=4, t=PACK)
            src = o32[a][:, :, start : start + width].rearrange("p t (c i) -> p c t i", i=4)
            if on_vector:
                nc.vector.tensor_copy(out=dst, in_=src)
            else:
                nc.scalar.copy(out=dst, in_=src)

        def planes(a):
            cols = slice(a * HALF, (a + 1) * HALF)
            o_words = new([P, HALF], U32, f"o_words{a}")
            nc.vector.quantize_mx(out=o_words[:].bitcast(FP8X4), scales=o_scales[:, cols], in_=o_bf[a][:])
            nc.sync.dma_start(out=out_words[:, cols], in_=o_words[:].bitcast(I32))

        for t in (0, 2, 1, 3):
            nc.vector.tensor_tensor(
                out=h_sum[0][:, t, :], in0=picked(h[t], n3_sb, 0, HALF), in1=h_first[:, t, :], op=ALU.add
            )
        gated(0)
        gated(1)
        nc.sync.dma_start(out=out_rows[:, :, :HALF], in_=o32[0][:])

        h_n3 = new([P, PACK, HALF], F32, "h_n3")
        for t in (0, 2, 1, 3):
            nc.scalar.activation(out=h_n3[:, t, :], in_=picked(h[t], n3_sb, HALF, HALF), func=ACT.Copy)
        gate(2)
        gate(3)
        nc.vector.scalar_tensor_tensor(
            out=h_sum[1][:, 0::2, :], in0=h_ps[1][0][:], scalar=0.5, in1=h_n3[:, 0::2, :],
            op0=ALU.mult, op1=ALU.add,
        )
        for t in (1, 3):
            nc.gpsimd.tensor_tensor(out=h_sum[1][:, t, :], in0=h_n3[:, t, :], in1=h[t][:, HALF:], op=ALU.add)
        rounded(0, 0, HALF, False)
        for b in range(2):
            gated(2 + b)
            nc.sync.dma_start(
                out=out_rows[:, :, HALF + b * P : HALF + (b + 1) * P], in_=o32[1][:, :, b * P : (b + 1) * P]
            )
        rounded(1, 0, P, False)
        planes(0)
        rounded(1, P, P, True)
        planes(1)
        for q in range(4):
            queue = nc.sync if q % 2 == 0 else nc.scalar
            queue.dma_start(
                out=out_2[0][4 * q : 4 * q + 4, :].bitcast(I32), in_=o_scales[32 * q : 32 * q + 4, :].bitcast(I32)
            )
